import numpy as np
import ml_dtypes


def mxq(x, axis, fmt="e4m3"):
    dtype, down = {"e4m3": (ml_dtypes.float8_e4m3fn, 7), "e5m2": (ml_dtypes.float8_e5m2, 14)}[fmt]
    v = np.moveaxis(np.asarray(x, np.float32).astype(ml_dtypes.bfloat16).astype(np.float64), axis, -1)
    blocks = v.reshape(v.shape[:-1] + (-1, 32))
    amax = np.abs(blocks).max(-1, keepdims=True)
    byte = np.maximum(np.where(amax > 0, np.frexp(amax)[1] - 1 + 127, 0) - down, 1)
    scale = np.exp2(byte - 127.0)
    codes = (blocks / scale).astype(np.float32).astype(dtype).astype(np.float64)
    return np.moveaxis((codes * scale).reshape(v.shape), -1, axis)


WIDE = False


def mx_kscale(k):
    if not WIDE:
        return np.ones(k)
    levels = np.array([10, -10, 5, -5, 0])
    if k % 512:
        return np.exp2(np.random.permutation(np.resize(levels, k // 32))).repeat(32)
    a = np.empty((k // 512, 16))
    for p in range(k // 512):
        a[p, :8] = np.random.permutation(np.resize(levels, 8))
        for g in range(8):
            far = levels[np.abs(levels - a[p, g]) >= 10]
            a[p, g + 8] = far[np.random.randint(len(far))]
    return np.exp2(a.ravel()).repeat(32)


def f64(x):
    return np.asarray(x).astype(np.float64)


def striped(idx):
    return np.tile(idx.reshape(-1, 16).T, (8, 1)).astype(np.uint16)


def unstriped(offs):
    return offs[:16].T.reshape(-1).astype(np.int64)


E2M1 = np.array([0.0, 0.5, 1.0, 1.5, 2.0, 3.0, 4.0, 6.0, -0.0, -0.5, -1.0, -1.5, -2.0, -3.0, -4.0, -6.0])


def pack_weight(w, fmt):
    k, n = w.shape
    w = f64(np.asarray(w, np.float32).astype(ml_dtypes.bfloat16)).reshape(k // 32, 32, n)
    amax = np.abs(w).max(1)
    if fmt == "e4m3":
        byte = np.frexp(amax)[1] - 1 + 127 - 7
    else:
        mant, ex = np.frexp(amax / 6.0)
        byte = np.where(mant > 0.5, ex, ex - 1) + 127
    byte = np.clip(np.where(amax > 0, byte, 1), 1, 254)
    scaled = (w * np.exp2(127.0 - byte)[:, None, :]).reshape(k, n).astype(np.float32)
    by_word = np.ascontiguousarray(scaled.reshape(k // 512, 128, 4, n).transpose(0, 1, 3, 2))
    if fmt == "e4m3":
        words = by_word.astype(ml_dtypes.float8_e4m3fn).view(np.uint8)
    else:
        c = by_word.astype(ml_dtypes.float4_e2m1fn).view(np.uint8) & 0xF
        words = (c[..., 0::2] | (c[..., 1::2] << 4)).reshape(k // 512, 128, 2 * n)
    return np.ascontiguousarray(words), np.ascontiguousarray(byte.astype(np.uint8).reshape(k // 512, 16, n))


def unpack_weight(words, scales, fmt):
    g, _, n = scales.shape
    words = np.ascontiguousarray(words).reshape(g, 128, n, -1)
    if fmt == "e4m3":
        vals = words.view(ml_dtypes.float8_e4m3fn).astype(np.float64)
    else:
        nib = np.empty((g, 128, n, 4), np.uint8)
        nib[..., 0::2] = words & 0xF
        nib[..., 1::2] = words >> 4
        vals = E2M1[nib]
    vals = vals * np.repeat(np.exp2(scales.astype(np.float64) - 127.0), 8, axis=1)[..., None]
    return vals.transpose(0, 1, 3, 2).reshape(g * 512, n)


def gelu(v):
    return 0.5 * v * (1.0 + np.tanh(np.sqrt(2.0 / np.pi) * (v + 0.044715 * v**3)))


def striped8(idx):
    return np.concatenate([v.reshape(-1, 16).T for v in idx]).astype(np.uint16)


def unstriped8(offs):
    return np.stack([offs[16 * g:16 * g + 16].T.reshape(-1) for g in range(8)]).astype(np.int64)


def runs(v, idx8):
    k = np.arange(v.shape[0])
    return v[k[:, None], idx8[k % 512 // 64]]


def bf(x):
    return np.asarray(x, np.float32).astype(ml_dtypes.bfloat16)


def planes(Y):
    n, m = Y.shape
    b = f64(bf(Y)).reshape(n // 32, 32, m)
    amax = np.abs(b).max(1)
    byte = np.clip(np.where(amax > 0, np.frexp(amax)[1] - 1 + 127 - 7, 1), 1, 254)
    codes = (b * np.exp2(127.0 - byte)[:, None, :]).reshape(n, m).astype(np.float32).astype(ml_dtypes.float8_e4m3fn).view(np.uint8)
    words = codes.reshape(n // 512, 128, 4, m).transpose(0, 1, 3, 2)
    return np.ascontiguousarray(words), np.ascontiguousarray(byte.astype(np.uint8).reshape(n // 512, 16, m))


K, H, N, T, S, P = 1536, 1024, 1024, 2048, 1024, 512

def setup_inputs():
    n = np.random.standard_normal
    s = mx_kscale(K)[:, None]
    u = mx_kscale(H)[:, None]
    d = {}
    d["tab_words"], d["tab_scales"] = pack_weight(n((K, T)) * s, "e4m3")
    d["offs"] = striped8(np.stack([np.random.permutation(T)[:S] for _ in range(8)]))
    d["pos1"] = striped(np.random.permutation(S)[:P])
    d["pos2"] = striped(np.random.permutation(S)[:P])
    d["w1"] = (0.38 * n((K, H)) / K ** 0.5 / s).astype(np.float32)
    d["ref"] = np.random.uniform(-1.1, 1.1, (H, S)).astype(np.float32)
    d["gain"] = (1.5 * np.exp(0.3 * n(H)) * u[:, 0]).astype(np.float32)
    w4 = n((H, N)) / H ** 0.5 * np.exp(0.8 * n(N))[None, :] / u
    d["w4_words"], d["w4_scales"] = pack_weight(w4, "e2m1")
    return d

def reference(tab_words, tab_scales, offs, pos1, pos2, w1, ref, gain, w4_words, w4_scales):
    v = runs(unpack_weight(tab_words, tab_scales, "e4m3"), unstriped8(offs))
    h = np.abs((mxq(f64(w1), 0, "e4m3").T @ v) - f64(ref))
    h1 = h[:, unstriped(pos1)]
    h2 = h[:, unstriped(pos2)]
    x = f64(gain)[:, None] * (h1 * np.cos(h2) - h2)
    w4 = unpack_weight(w4_words, w4_scales, "e2m1")
    y = w4.T @ mxq(x, 0, "e4m3")
    words, scales = planes(y)
    return y, words, scales

@@ -1,0 +1,328 @@
+import math
+from contextlib import ExitStack
+
+import concourse.mybir as mybir
+
+K, H, N, T, S, PAIRS = 1536, 1024, 1024, 2048, 1024, 512
+FLOPS = 2 * K * H * S + 2 * H * N * PAIRS
+
+F32 = mybir.dt.float32
+BF16 = mybir.dt.bfloat16
+I32 = mybir.dt.int32
+U32 = mybir.dt.uint32
+U16 = mybir.dt.uint16
+U8 = mybir.dt.uint8
+E4M3X4 = mybir.dt.float8_e4m3fn_x4
+E2M1X4 = mybir.dt.float4_e2m1fn_x4
+ALU = mybir.AluOpType
+ACT = mybir.ActivationFunctionType
+
+P = 128
+PACK = 4
+PASS = P * PACK
+K_PASSES = K // PASS
+H_PASSES = H // PASS
+N_GROUPS = N // PASS
+BANK = 512
+SCALE_ROW0 = 10
+TINY = 2.0 ** -100
+PIECES = ((0, 256), (256, 512))
+
+
+def tile_list_perimetry_visit_features_kernel(
+    tc, tab_words, tab_scales, offs, pos1, pos2, w1, ref, gain, w4_words, w4_scales, out_0, out_1, out_2
+):
+    nc = tc.nc
+    with ExitStack() as ctx:
+        keep = ctx.enter_context(tc.tile_pool(name="keep", bufs=1))
+        stage = ctx.enter_context(tc.tile_pool(name="stage", bufs=4))
+        h_pool = ctx.enter_context(tc.tile_pool(name="h", bufs=8))
+        work = ctx.enter_context(tc.tile_pool(name="work", bufs=3))
+        psum = ctx.enter_context(tc.psum_pool(name="psum", bufs=4))
+
+        offs_sb = keep.tile([P, S // 16], U16, name="offs_sb")
+        pos1_sb = keep.tile([P, PAIRS // 16], U16, name="pos1_sb")
+        pos2_sb = keep.tile([P, PAIRS // 16], U16, name="pos2_sb")
+        nc.sync.dma_start(offs_sb[:], offs)
+        nc.sync.dma_start(pos2_sb[:], pos2)
+        nc.sync.dma_start(pos1_sb[:], pos1)
+        gain_sb = keep.tile([P, H_PASSES, PACK], F32, name="gain_sb")
+
+        ones = stage.tile([P, 1], F32, name="stage", align_bytes=64)
+        nc.gpsimd.memset(ones[:], 1.0)
+
+        scale_win = keep.tile([P, T], U8, name="scale_win", align_bytes=64)
+        scale_got = keep.tile([P, S], U8, name="scale_got", align_bytes=64)
+        v_scales = keep.tile([P, K_PASSES, S], U8, name="v_scales", align_bytes=64)
+        nc.gpsimd.memset(scale_win[:].bitcast(I32), 0)
+        rows = PACK * K_PASSES
+        for d in range(4):
+            lo = 32 * d + SCALE_ROW0
+            nc.sync.dma_start(
+                out=scale_win[lo : lo + rows, :].bitcast(I32),
+                in_=tab_scales[:, 4 * d : 4 * d + 4, :].rearrange("a r t -> r a t").bitcast(I32),
+            )
+        nc.vector.memset(v_scales[:].rearrange("p a s -> p (a s)").bitcast(I32), 0)
+
+        nc.vector.tensor_copy(scale_got[:], scale_win[:].indirect(offs_sb[:]))
+        for d in range(4):
+            lo = 32 * d + SCALE_ROW0
+            nc.sync.dma_start(
+                out=v_scales[32 * d : 32 * d + 4].rearrange("p a s -> p (a s)").bitcast(I32),
+                in_=scale_got[lo : lo + rows, :].bitcast(I32),
+            )
+
+        nc.gpsimd.dma_start(out=gain_sb[:], in_=gain.rearrange("(b p t) -> p b t", p=P, t=PACK))
+
+        w4s_raw = keep.tile([P, H_PASSES, N], U8, name="w4s_raw", align_bytes=64)
+        w4s = keep.tile([P, H_PASSES, N], U8, name="w4s", align_bytes=64)
+        nc.vector.memset(w4s_raw[:].rearrange("p a n -> p (a n)").bitcast(I32), 0)
+        for q in range(4):
+            nc.gpsimd.dma_start(
+                out=w4s_raw[32 * q : 32 * q + 4].rearrange("p a n -> p (a n)").bitcast(I32),
+                in_=w4_scales[:, 4 * q : 4 * q + 4, :].rearrange("a r n -> r a n").bitcast(I32),
+            )
+
+        w1_codes = {}
+        w1_scales = {}
+        w1_raw = {}
+        w1_grouped = {}
+
+        def load_w1(a, b):
+            raw = stage.tile([P, PACK, PASS], F32, name="stage", align_bytes=64)
+            nc.sync.dma_start(
+                out=raw[:],
+                in_=w1[a * PASS : (a + 1) * PASS, b * PASS : (b + 1) * PASS].rearrange("(p j) c -> p j c", j=PACK),
+            )
+            w1_raw[a, b] = raw
+
+        def round_w1(a, b, on_vector):
+            grouped = work.tile([P, PACK, P, PACK], BF16, name="w1_grouped", align_bytes=64)
+            src = w1_raw[a, b][:].rearrange("p j (m t) -> p m j t", t=PACK)
+            dst = grouped[:].rearrange("p t m j -> p m j t")
+            if on_vector:
+                nc.vector.tensor_copy(out=dst, in_=src)
+            else:
+                nc.scalar.copy(out=dst, in_=src)
+            w1_grouped[a, b] = grouped
+
+        def quantise_w1(a, b):
+            codes = keep.tile([P, PASS], U32, name="w1_codes_%d_%d" % (a, b), align_bytes=64)
+            scales = keep.tile([P, PASS], U8, name="w1_scales_%d_%d" % (a, b), align_bytes=64)
+            nc.vector.quantize_mx(
+                out=codes[:].bitcast(E4M3X4),
+                scales=scales[:],
+                in_=w1_grouped[a, b][:].rearrange("p t m j -> p (t m j)"),
+            )
+            w1_codes[a, b] = codes
+            w1_scales[a, b] = scales
+
+        v_words = []
+        tabs = []
+
+        def load_table(a):
+            tab = stage.tile([P, T], I32, name="stage", align_bytes=64)
+            nc.sync.dma_start(out=tab[:], in_=tab_words[a].rearrange("p t i -> p (t i)").bitcast(I32))
+            tabs.append(tab)
+
+        load_table(0)
+        load_w1(0, 0)
+        load_w1(1, 0)
+        neg_pi = keep.tile([P, 1], F32, name="neg_pi")
+        nc.vector.tensor_scalar(out=neg_pi[:], in0=ones[:], scalar1=-math.pi, scalar2=None, op0=ALU.mult)
+        load_table(1)
+        load_table(2)
+        load_w1(2, 0)
+        for a in range(K_PASSES):
+            got = keep.tile([P, S], U32, name="v_words_%d" % a, align_bytes=64)
+            nc.vector.tensor_copy(got[:], tabs[a][:].bitcast(U32).indirect(offs_sb[:]))
+            v_words.append(got)
+            round_w1(a, 0, a == K_PASSES - 1)
+            quantise_w1(a, 0)
+
+        ref_sb = {}
+
+        def load_ref(b, t0):
+            tile = stage.tile([P, 2, S], F32, name="stage", align_bytes=64)
+            nc.sync.dma_start(
+                out=tile[:],
+                in_=ref[b * PASS : (b + 1) * PASS, :].rearrange("(p t) j -> p t j", t=PACK)[:, t0 : t0 + 2, :],
+            )
+            ref_sb[b, t0] = tile[:, 0, :]
+            ref_sb[b, t0 + 1] = tile[:, 1, :]
+
+        load_ref(0, 0)
+        load_ref(0, 2)
+        for a in range(K_PASSES):
+            load_w1(a, 1)
+        load_ref(1, 0)
+        load_ref(1, 2)
+        w4_raw = stage.tile([P, H_PASSES, N // 2], I32, name="stage", align_bytes=64)
+        nc.sync.dma_start(out=w4_raw[:], in_=w4_words.rearrange("a p c -> p a c").bitcast(I32))
+
+        gains = gain_sb[:].rearrange("p b t -> p (b t)")
+        cols = H_PASSES * PACK
+        sgn = keep.tile([P, cols], F32, name="sgn")
+        neg_sgn = keep.tile([P, cols], F32, name="neg_sgn")
+        sin_bias = keep.tile([P, cols], F32, name="sin_bias")
+        mag = keep.tile([P, cols], F32, name="mag")
+        inv_mag = keep.tile([P, cols], F32, name="inv_mag")
+        nc.vector.tensor_scalar(out=sgn[:], in0=gains, scalar1=0.0, scalar2=2.0, op0=ALU.is_ge, op1=ALU.mult)
+        nc.vector.tensor_scalar(out=neg_sgn[:], in0=sgn[:], scalar1=-1.0, scalar2=1.0, op0=ALU.mult, op1=ALU.add)
+        nc.vector.tensor_scalar(out=sgn[:], in0=sgn[:], scalar1=-1.0, scalar2=None, op0=ALU.add)
+        nc.vector.tensor_scalar(out=sin_bias[:], in0=neg_sgn[:], scalar1=math.pi / 2, scalar2=None, op0=ALU.mult)
+        nc.vector.tensor_tensor(out=mag[:], in0=gains, in1=sgn[:], op=ALU.mult)
+        nc.vector.tensor_scalar(out=mag[:], in0=mag[:], scalar1=TINY, scalar2=None, op0=ALU.max)
+        nc.vector.reciprocal(out=inv_mag[:], in_=mag[:])
+
+        w4_dealt = keep.tile([P, H_PASSES, N], U16, name="w4_dealt", align_bytes=64)
+        nc.scalar.copy(
+            out=w4_dealt[:].rearrange("p a (g t m) -> p (a g) m t", g=N_GROUPS, t=PACK),
+            in_=w4_raw[:].bitcast(U16).rearrange("p a (g m t) -> p (a g) m t", g=N_GROUPS, t=PACK),
+        )
+
+        h_sb = {}
+
+        def first_stage(b, t):
+            h = h_pool.tile([P, S], F32, name="h_sb")
+            m_cols = slice(t * P, (t + 1) * P)
+            for j0 in range(0, S, BANK):
+                acc = psum.tile([P, BANK], F32, name="acc1")
+                for a in range(K_PASSES):
+                    nc.tensor.matmul_mx(
+                        out=acc[:],
+                        lhsT=w1_codes[a, b][:, m_cols].bitcast(E4M3X4),
+                        lhsT_scale=w1_scales[a, b][:, m_cols],
+                        rhs=v_words[a][:, j0 : j0 + BANK].bitcast(E4M3X4),
+                        rhs_scale=v_scales[:, a, j0 : j0 + BANK],
+                        start=(a == 0),
+                        stop=(a == K_PASSES - 1),
+                    )
+                nc.vector.tensor_tensor(
+                    out=h[:, j0 : j0 + BANK], in0=acc[:], in1=ref_sb[b, t][:, j0 : j0 + BANK], op=ALU.subtract
+                )
+            col = b * PACK + t
+            nc.scalar.activation(out=h[:], in_=h[:], func=ACT.Abs, scale=gains[:, col : col + 1])
+            h_sb[b, t] = h
+
+        follow = {}
+        cosine = {}
+
+        def pick_follow_up(b, t, lo, hi):
+            col = b * PACK + t
+            h2 = work.tile([P, hi - lo], F32, name="h2")
+            nc.vector.tensor_copy(h2[:], h_sb[b, t][:].indirect(pos2_sb[:, lo // 16 : hi // 16]))
+            cos = work.tile([P, hi - lo], F32, name="cos")
+            nc.scalar.activation(out=cos[:], in_=h2[:], func=ACT.Abs, scale=inv_mag[:, col : col + 1], bias=neg_pi[:])
+            nc.scalar.activation(
+                out=cos[:], in_=cos[:], func=ACT.Sin, scale=sgn[:, col : col + 1], bias=sin_bias[:, col : col + 1]
+            )
+            follow[b, t, lo] = h2
+            cosine[b, t, lo] = cos
+
+        def combine(b, t, lo, hi, x32):
+            col = b * PACK + t
+            prod = work.tile([P, hi - lo], F32, name="prod")
+            nc.vector.tensor_tensor(
+                prod[:], h_sb[b, t][:].indirect(pos1_sb[:, lo // 16 : hi // 16]), cosine[b, t, lo][:], ALU.mult
+            )
+            nc.vector.scalar_tensor_tensor(
+                out=x32[:, t, :],
+                in0=follow[b, t, lo][:],
+                scalar=neg_sgn[:, col : col + 1],
+                in1=prod[:],
+                op0=ALU.mult,
+                op1=ALU.add,
+            )
+
+        def interleave(engine_copy, dst, src):
+            engine_copy(
+                out=dst[:].rearrange("p (c i) t -> p c t i", i=PACK),
+                in_=src[:].rearrange("p t (c i) -> p c t i", i=PACK),
+            )
+
+        def quantise_x(b, lo, hi, x32):
+            x16 = work.tile([P, hi - lo, PACK], BF16, name="x16", align_bytes=64)
+            interleave(nc.scalar.copy, x16, x32)
+            codes = keep.tile([P, hi - lo], U32, name="x_codes_%d_%d" % (b, lo), align_bytes=64)
+            scales = keep.tile([P, hi - lo], U8, name="x_scales_%d_%d" % (b, lo), align_bytes=64)
+            nc.vector.quantize_mx(
+                out=codes[:].bitcast(E4M3X4), scales=scales[:], in_=x16[:].rearrange("p c t -> p (c t)")
+            )
+            return codes, scales
+
+        y_scales = keep.tile([P, N_GROUPS, PAIRS], U8, name="y_scales", align_bytes=64)
+
+        def second_stage(lo, hi, operands, last):
+            width = hi - lo
+            for g in range(N_GROUPS):
+                y = stage.tile([P, PACK, width], F32, name="stage", align_bytes=64)
+                for t0 in range(0, PACK, 2):
+                    acc = psum.tile([P, 2, width], F32, name="acc2")
+                    for t in range(t0, t0 + 2):
+                        n_cols = slice(g * PASS + t * P, g * PASS + (t + 1) * P)
+                        for b in range(H_PASSES):
+                            codes, scales = operands[b]
+                            nc.tensor.matmul_mx(
+                                out=acc[:, t - t0, :],
+                                lhsT=w4_dealt[:, b, n_cols].bitcast(E2M1X4),
+                                lhsT_scale=w4s[:, b, n_cols],
+                                rhs=codes.bitcast(E4M3X4),
+                                rhs_scale=scales,
+                                start=(b == 0),
+                                stop=(b == H_PASSES - 1),
+                            )
+                    nc.scalar.copy(out=y[:, t0 : t0 + 2, :], in_=acc[:])
+                nc.sync.dma_start(
+                    out=out_0[g * PASS : (g + 1) * PASS, lo:hi].rearrange("(p t) j -> p t j", t=PACK), in_=y[:]
+                )
+                y16 = work.tile([P, width, PACK], BF16, name="y16", align_bytes=64)
+                interleave(nc.vector.tensor_copy if last else nc.scalar.copy, y16, y)
+                y_codes = work.tile([P, width], U32, name="y_codes", align_bytes=64)
+                nc.vector.quantize_mx(
+                    out=y_codes[:].bitcast(E4M3X4),
+                    scales=y_scales[:, g, lo:hi],
+                    in_=y16[:].rearrange("p c t -> p (c t)"),
+                )
+                nc.sync.dma_start(
+                    out=out_1[g].rearrange("p m t -> p (m t)").bitcast(I32)[:, lo:hi], in_=y_codes[:].bitcast(I32)
+                )
+
+        x32 = work.tile([P, PACK, PAIRS], F32, name="x32")
+        first_stage(0, 0)
+        first_stage(0, 1)
+        pick_follow_up(0, 0, 0, PAIRS)
+        for t in range(PACK):
+            if t + 2 < PACK:
+                first_stage(0, t + 2)
+            if t + 1 < PACK:
+                pick_follow_up(0, t + 1, 0, PAIRS)
+            if t < K_PASSES:
+                round_w1(t, 1, False)
+            combine(0, t, 0, PAIRS, x32)
+            if t < K_PASSES:
+                quantise_w1(t, 1)
+        nc.vector.tensor_copy(
+            out=w4s[:].rearrange("p a (g t m) -> p (a g) m t", g=N_GROUPS, t=PACK),
+            in_=w4s_raw[:].rearrange("p a (g m t) -> p (a g) m t", g=N_GROUPS, t=PACK),
+        )
+        for t in range(PACK):
+            first_stage(1, t)
+        x_codes0, x_scales0 = quantise_x(0, 0, PAIRS, x32)
+
+        for lo, hi in PIECES:
+            x32 = work.tile([P, PACK, hi - lo], F32, name="x32")
+            pick_follow_up(1, 0, lo, hi)
+            for t in range(PACK):
+                if t + 1 < PACK:
+                    pick_follow_up(1, t + 1, lo, hi)
+                combine(1, t, lo, hi, x32)
+            codes, scales = quantise_x(1, lo, hi, x32)
+            second_stage(lo, hi, ((x_codes0[:, lo:hi], x_scales0[:, lo:hi]), (codes[:], scales[:])), hi == PAIRS)
+
+        for q in range(4):
+            queue = nc.sync if q % 2 == 0 else nc.scalar
+            queue.dma_start(
+                out=out_2[:, 4 * q : 4 * q + 4, :].rearrange("g r m -> r g m").bitcast(I32),
+                in_=y_scales[32 * q : 32 * q + 4].rearrange("p g m -> p (g m)").bitcast(I32),
+            )

@@ -37,7 +37,8 @@ def tile_list_perimetry_visit_features_kernel(
         keep = ctx.enter_context(tc.tile_pool(name="keep", bufs=1))
         stage = ctx.enter_context(tc.tile_pool(name="stage", bufs=4))
         h_pool = ctx.enter_context(tc.tile_pool(name="h", bufs=8))
-        work = ctx.enter_context(tc.tile_pool(name="work", bufs=3))
+        work = ctx.enter_context(tc.tile_pool(name="work", bufs=2))
+        picks = ctx.enter_context(tc.tile_pool(name="picks", bufs=4))
         psum = ctx.enter_context(tc.psum_pool(name="psum", bufs=4))
 
         offs_sb = keep.tile([P, S // 16], U16, name="offs_sb")
@@ -46,10 +47,11 @@ def tile_list_perimetry_visit_features_kernel(
         nc.sync.dma_start(offs_sb[:], offs)
         nc.sync.dma_start(pos2_sb[:], pos2)
         nc.sync.dma_start(pos1_sb[:], pos1)
-        gain_sb = keep.tile([P, H_PASSES, PACK], F32, name="gain_sb")
 
         ones = stage.tile([P, 1], F32, name="stage", align_bytes=64)
         nc.gpsimd.memset(ones[:], 1.0)
+        gain_sb = stage.tile([P, H_PASSES, PACK], F32, name="stage", align_bytes=64)
+        nc.sync.dma_start(out=gain_sb[:], in_=gain.rearrange("(b p t) -> p b t", p=P, t=PACK))
 
         scale_win = keep.tile([P, T], U8, name="scale_win", align_bytes=64)
         scale_got = keep.tile([P, S], U8, name="scale_got", align_bytes=64)
@@ -67,15 +69,12 @@ def tile_list_perimetry_visit_features_kernel(
         nc.vector.tensor_copy(scale_got[:], scale_win[:].indirect(offs_sb[:]))
         for d in range(4):
             lo = 32 * d + SCALE_ROW0
-            nc.sync.dma_start(
+            nc.gpsimd.dma_start(
                 out=v_scales[32 * d : 32 * d + 4].rearrange("p a s -> p (a s)").bitcast(I32),
                 in_=scale_got[lo : lo + rows, :].bitcast(I32),
             )
 
-        nc.gpsimd.dma_start(out=gain_sb[:], in_=gain.rearrange("(b p t) -> p b t", p=P, t=PACK))
-
         w4s_raw = keep.tile([P, H_PASSES, N], U8, name="w4s_raw", align_bytes=64)
-        w4s = keep.tile([P, H_PASSES, N], U8, name="w4s", align_bytes=64)
         nc.vector.memset(w4s_raw[:].rearrange("p a n -> p (a n)").bitcast(I32), 0)
         for q in range(4):
             nc.gpsimd.dma_start(
@@ -96,14 +95,11 @@ def tile_list_perimetry_visit_features_kernel(
             )
             w1_raw[a, b] = raw
 
-        def round_w1(a, b, on_vector):
-            grouped = work.tile([P, PACK, P, PACK], BF16, name="w1_grouped", align_bytes=64)
+        def round_w1(a, b):
+            grouped = picks.tile([P, PACK, P, PACK], BF16, name="w1_grouped", align_bytes=64)
             src = w1_raw[a, b][:].rearrange("p j (m t) -> p m j t", t=PACK)
             dst = grouped[:].rearrange("p t m j -> p m j t")
-            if on_vector:
-                nc.vector.tensor_copy(out=dst, in_=src)
-            else:
-                nc.scalar.copy(out=dst, in_=src)
+            nc.scalar.copy(out=dst, in_=src)
             w1_grouped[a, b] = grouped
 
         def quantise_w1(a, b):
@@ -127,39 +123,8 @@ def tile_list_perimetry_visit_features_kernel(
 
         load_table(0)
         load_w1(0, 0)
-        load_w1(1, 0)
         neg_pi = keep.tile([P, 1], F32, name="neg_pi")
         nc.vector.tensor_scalar(out=neg_pi[:], in0=ones[:], scalar1=-math.pi, scalar2=None, op0=ALU.mult)
-        load_table(1)
-        load_table(2)
-        load_w1(2, 0)
-        for a in range(K_PASSES):
-            got = keep.tile([P, S], U32, name="v_words_%d" % a, align_bytes=64)
-            nc.vector.tensor_copy(got[:], tabs[a][:].bitcast(U32).indirect(offs_sb[:]))
-            v_words.append(got)
-            round_w1(a, 0, a == K_PASSES - 1)
-            quantise_w1(a, 0)
-
-        ref_sb = {}
-
-        def load_ref(b, t0):
-            tile = stage.tile([P, 2, S], F32, name="stage", align_bytes=64)
-            nc.sync.dma_start(
-                out=tile[:],
-                in_=ref[b * PASS : (b + 1) * PASS, :].rearrange("(p t) j -> p t j", t=PACK)[:, t0 : t0 + 2, :],
-            )
-            ref_sb[b, t0] = tile[:, 0, :]
-            ref_sb[b, t0 + 1] = tile[:, 1, :]
-
-        load_ref(0, 0)
-        load_ref(0, 2)
-        for a in range(K_PASSES):
-            load_w1(a, 1)
-        load_ref(1, 0)
-        load_ref(1, 2)
-        w4_raw = stage.tile([P, H_PASSES, N // 2], I32, name="stage", align_bytes=64)
-        nc.sync.dma_start(out=w4_raw[:], in_=w4_words.rearrange("a p c -> p a c").bitcast(I32))
-
         gains = gain_sb[:].rearrange("p b t -> p (b t)")
         cols = H_PASSES * PACK
         sgn = keep.tile([P, cols], F32, name="sgn")
@@ -175,10 +140,66 @@ def tile_list_perimetry_visit_features_kernel(
         nc.vector.tensor_scalar(out=mag[:], in0=mag[:], scalar1=TINY, scalar2=None, op0=ALU.max)
         nc.vector.reciprocal(out=inv_mag[:], in_=mag[:])
 
+        load_table(1)
+        load_w1(1, 0)
+        load_table(2)
+        load_w1(2, 0)
+        for a in range(K_PASSES):
+            got = keep.tile([P, S], U32, name="v_words_%d" % a, align_bytes=64)
+            nc.vector.tensor_copy(got[:], tabs[a][:].bitcast(U32).indirect(offs_sb[:]))
+            v_words.append(got)
+            if a < K_PASSES - 1:
+                round_w1(a, 0)
+                quantise_w1(a, 0)
+        last = K_PASSES - 1
+        codes = keep.tile([P, PASS], U32, name="w1_codes_last", align_bytes=64)
+        scales = keep.tile([P, PASS], U8, name="w1_scales_last", align_bytes=64)
+        for half in range(2):
+            grouped = keep.tile([P, 2, P, PACK], BF16, name="w1_half_%d" % half, align_bytes=64)
+            nc.scalar.copy(
+                out=grouped[:].rearrange("p t m j -> p m j t"),
+                in_=w1_raw[last, 0][:].rearrange("p j (m t) -> p m j t", t=PACK)[:, :, :, 2 * half : 2 * half + 2],
+            )
+            half_cols = slice(half * 2 * P, (half + 1) * 2 * P)
+            nc.vector.quantize_mx(
+                out=codes[:, half_cols].bitcast(E4M3X4),
+                scales=scales[:, half_cols],
+                in_=grouped[:].rearrange("p t m j -> p (t m j)"),
+            )
+        w1_codes[last, 0] = codes
+        w1_scales[last, 0] = scales
+
+        ref_sb = {}
+
+        def load_ref(b, t0):
+            tile = stage.tile([P, 2, S], F32, name="stage", align_bytes=64)
+            nc.sync.dma_start(
+                out=tile[:],
+                in_=ref[b * PASS : (b + 1) * PASS, :].rearrange("(p t) j -> p t j", t=PACK)[:, t0 : t0 + 2, :],
+            )
+            ref_sb[b, t0] = tile[:, 0, :]
+            ref_sb[b, t0 + 1] = tile[:, 1, :]
+
+        w4_raw = stage.tile([P, H_PASSES, N // 2], I32, name="stage", align_bytes=64)
+        nc.sync.dma_start(out=w4_raw[:], in_=w4_words.rearrange("a p c -> p a c").bitcast(I32))
+        load_ref(0, 0)
+        load_w1(0, 1)
+        load_ref(0, 2)
+        load_w1(1, 1)
+        load_w1(2, 1)
+        load_ref(1, 0)
+        load_ref(1, 2)
+
         w4_dealt = keep.tile([P, H_PASSES, N], U16, name="w4_dealt", align_bytes=64)
         nc.scalar.copy(
             out=w4_dealt[:].rearrange("p a (g t m) -> p (a g) m t", g=N_GROUPS, t=PACK),
             in_=w4_raw[:].bitcast(U16).rearrange("p a (g m t) -> p (a g) m t", g=N_GROUPS, t=PACK),
+        )
+
+        w4s = keep.tile([P, H_PASSES, N], U8, name="w1_half_0", align_bytes=64)
+        nc.vector.tensor_copy(
+            out=w4s[:].rearrange("p a (g t m) -> p (a g) m t", g=N_GROUPS, t=PACK),
+            in_=w4s_raw[:].rearrange("p a (g m t) -> p (a g) m t", g=N_GROUPS, t=PACK),
         )
 
         h_sb = {}
@@ -202,35 +223,34 @@ def tile_list_perimetry_visit_features_kernel(
                     out=h[:, j0 : j0 + BANK], in0=acc[:], in1=ref_sb[b, t][:, j0 : j0 + BANK], op=ALU.subtract
                 )
             col = b * PACK + t
-            nc.scalar.activation(out=h[:], in_=h[:], func=ACT.Abs, scale=gains[:, col : col + 1])
+            nc.scalar.activation(out=h[:], in_=h[:], func=ACT.Abs, scale=mag[:, col : col + 1])
             h_sb[b, t] = h
 
         follow = {}
         cosine = {}
 
-        def pick_follow_up(b, t, lo, hi):
+        def pick_follow_up(b, t):
             col = b * PACK + t
-            h2 = work.tile([P, hi - lo], F32, name="h2")
-            nc.vector.tensor_copy(h2[:], h_sb[b, t][:].indirect(pos2_sb[:, lo // 16 : hi // 16]))
-            cos = work.tile([P, hi - lo], F32, name="cos")
+            h2 = picks.tile([P, PAIRS], F32, name="h2")
+            nc.vector.tensor_copy(h2[:], h_sb[b, t][:].indirect(pos2_sb[:]))
+            cos = picks.tile([P, PAIRS], F32, name="cos")
             nc.scalar.activation(out=cos[:], in_=h2[:], func=ACT.Abs, scale=inv_mag[:, col : col + 1], bias=neg_pi[:])
             nc.scalar.activation(
                 out=cos[:], in_=cos[:], func=ACT.Sin, scale=sgn[:, col : col + 1], bias=sin_bias[:, col : col + 1]
             )
-            follow[b, t, lo] = h2
-            cosine[b, t, lo] = cos
+            follow[b, t] = h2
+            cosine[b, t] = cos
 
-        def combine(b, t, lo, hi, x32):
+        def combine(b, t, lo, hi, prod, x32):
             col = b * PACK + t
-            prod = work.tile([P, hi - lo], F32, name="prod")
             nc.vector.tensor_tensor(
-                prod[:], h_sb[b, t][:].indirect(pos1_sb[:, lo // 16 : hi // 16]), cosine[b, t, lo][:], ALU.mult
+                prod, h_sb[b, t][:].indirect(pos1_sb[:, lo // 16 : hi // 16]), cosine[b, t][:, lo:hi], ALU.mult
             )
             nc.vector.scalar_tensor_tensor(
                 out=x32[:, t, :],
-                in0=follow[b, t, lo][:],
+                in0=follow[b, t][:, lo:hi],
                 scalar=neg_sgn[:, col : col + 1],
-                in1=prod[:],
+                in1=prod,
                 op0=ALU.mult,
                 op1=ALU.add,
             )
@@ -243,7 +263,7 @@ def tile_list_perimetry_visit_features_kernel(
 
         def quantise_x(b, lo, hi, x32):
             x16 = work.tile([P, hi - lo, PACK], BF16, name="x16", align_bytes=64)
-            interleave(nc.scalar.copy, x16, x32)
+            interleave(nc.scalar.copy if b == 0 else nc.vector.tensor_copy, x16, x32)
             codes = keep.tile([P, hi - lo], U32, name="x_codes_%d_%d" % (b, lo), align_bytes=64)
             scales = keep.tile([P, hi - lo], U8, name="x_scales_%d_%d" % (b, lo), align_bytes=64)
             nc.vector.quantize_mx(
@@ -272,7 +292,8 @@ def tile_list_perimetry_visit_features_kernel(
                                 start=(b == 0),
                                 stop=(b == H_PASSES - 1),
                             )
-                    nc.scalar.copy(out=y[:, t0 : t0 + 2, :], in_=acc[:])
+                    evacuate = nc.vector.tensor_copy if last and t0 > 0 else nc.scalar.copy
+                    evacuate(out=y[:, t0 : t0 + 2, :], in_=acc[:])
                 nc.sync.dma_start(
                     out=out_0[g * PASS : (g + 1) * PASS, lo:hi].rearrange("(p t) j -> p t j", t=PACK), in_=y[:]
                 )
@@ -291,34 +312,41 @@ def tile_list_perimetry_visit_features_kernel(
         x32 = work.tile([P, PACK, PAIRS], F32, name="x32")
         first_stage(0, 0)
         first_stage(0, 1)
-        pick_follow_up(0, 0, 0, PAIRS)
+        pick_follow_up(0, 0)
         for t in range(PACK):
+            if t < K_PASSES:
+                round_w1(t, 1)
             if t + 2 < PACK:
                 first_stage(0, t + 2)
             if t + 1 < PACK:
-                pick_follow_up(0, t + 1, 0, PAIRS)
-            if t < K_PASSES:
-                round_w1(t, 1, False)
-            combine(0, t, 0, PAIRS, x32)
+                pick_follow_up(0, t + 1)
+            prod = work.tile([P, PAIRS], F32, name="prod")
+            combine(0, t, 0, PAIRS, prod[:], x32)
             if t < K_PASSES:
                 quantise_w1(t, 1)
-        nc.vector.tensor_copy(
-            out=w4s[:].rearrange("p a (g t m) -> p (a g) m t", g=N_GROUPS, t=PACK),
-            in_=w4s_raw[:].rearrange("p a (g m t) -> p (a g) m t", g=N_GROUPS, t=PACK),
-        )
-        for t in range(PACK):
-            first_stage(1, t)
+            if t == K_PASSES - 1:
+                first_stage(1, 0)
+                first_stage(1, 1)
+        pick_follow_up(1, 0)
         x_codes0, x_scales0 = quantise_x(0, 0, PAIRS, x32)
 
-        for lo, hi in PIECES:
-            x32 = work.tile([P, PACK, hi - lo], F32, name="x32")
-            pick_follow_up(1, 0, lo, hi)
-            for t in range(PACK):
-                if t + 1 < PACK:
-                    pick_follow_up(1, t + 1, lo, hi)
-                combine(1, t, lo, hi, x32)
-            codes, scales = quantise_x(1, lo, hi, x32)
-            second_stage(lo, hi, ((x_codes0[:, lo:hi], x_scales0[:, lo:hi]), (codes[:], scales[:])), hi == PAIRS)
+        (lo0, hi0), (lo1, hi1) = PIECES
+        x32 = work.tile([P, PACK, hi0 - lo0], F32, name="x32")
+        prods = keep.tile([P, PACK, hi0 - lo0], F32, name="prods")
+        for t in range(PACK):
+            if t + 2 < PACK:
+                first_stage(1, t + 2)
+            if t + 1 < PACK:
+                pick_follow_up(1, t + 1)
+            combine(1, t, lo0, hi0, prods[:, t, :], x32)
+        codes, scales = quantise_x(1, lo0, hi0, x32)
+        x32 = work.tile([P, PACK, hi1 - lo1], F32, name="x32")
+        prods = keep.tile([P, PACK, hi1 - lo1], F32, name="prods")
+        for t in range(PACK):
+            combine(1, t, lo1, hi1, prods[:, t, :], x32)
+        second_stage(lo0, hi0, ((x_codes0[:, lo0:hi0], x_scales0[:, lo0:hi0]), (codes[:], scales[:])), False)
+        codes, scales = quantise_x(1, lo1, hi1, x32)
+        second_stage(lo1, hi1, ((x_codes0[:, lo1:hi1], x_scales0[:, lo1:hi1]), (codes[:], scales[:])), True)
 
         for q in range(4):
             queue = nc.sync if q % 2 == 0 else nc.scalar

@@ -74,13 +74,13 @@ def tile_list_perimetry_visit_features_kernel(
                 in_=scale_got[lo : lo + rows, :].bitcast(I32),
             )
 
-        w4s_raw = keep.tile([P, H_PASSES, N], U8, name="w4s_raw", align_bytes=64)
-        nc.vector.memset(w4s_raw[:].rearrange("p a n -> p (a n)").bitcast(I32), 0)
-        for q in range(4):
-            nc.gpsimd.dma_start(
-                out=w4s_raw[32 * q : 32 * q + 4].rearrange("p a n -> p (a n)").bitcast(I32),
-                in_=w4_scales[:, 4 * q : 4 * q + 4, :].rearrange("a r n -> r a n").bitcast(I32),
-            )
+        w4s_raw = keep.tile([P, N], U8, name="w4s_raw", align_bytes=64)
+        w4s = keep.tile([P, H_PASSES, N], U8, name="w4s", align_bytes=64)
+        nc.vector.memset(w4s_raw[:].bitcast(I32), 0)
+        nc.gpsimd.dma_start(
+            out=w4s_raw[0 : 16 * H_PASSES, :].bitcast(I32), in_=w4_scales.rearrange("a q n -> q a n").bitcast(I32)
+        )
+        nc.vector.memset(w4s[:].rearrange("p a n -> p (a n)").bitcast(I32), 0)
 
         w1_codes = {}
         w1_scales = {}
@@ -180,27 +180,26 @@ def tile_list_perimetry_visit_features_kernel(
             ref_sb[b, t0] = tile[:, 0, :]
             ref_sb[b, t0 + 1] = tile[:, 1, :]
 
-        w4_raw = stage.tile([P, H_PASSES, N // 2], I32, name="stage", align_bytes=64)
-        nc.sync.dma_start(out=w4_raw[:], in_=w4_words.rearrange("a p c -> p a c").bitcast(I32))
         load_ref(0, 0)
         load_w1(0, 1)
         load_ref(0, 2)
         load_w1(1, 1)
         load_w1(2, 1)
         load_ref(1, 0)
+        w4_raw = stage.tile([P, H_PASSES, N // 2], I32, name="stage", align_bytes=64)
+        nc.sync.dma_start(out=w4_raw[:], in_=w4_words.rearrange("a p c -> p a c").bitcast(I32))
         load_ref(1, 2)
 
-        w4_dealt = keep.tile([P, H_PASSES, N], U16, name="w4_dealt", align_bytes=64)
-        nc.scalar.copy(
-            out=w4_dealt[:].rearrange("p a (g t m) -> p (a g) m t", g=N_GROUPS, t=PACK),
-            in_=w4_raw[:].bitcast(U16).rearrange("p a (g m t) -> p (a g) m t", g=N_GROUPS, t=PACK),
-        )
-
-        w4s = keep.tile([P, H_PASSES, N], U8, name="w1_half_0", align_bytes=64)
+        w4s_dealt = keep.tile([P, N], U8, name="w1_half_0", align_bytes=64)
         nc.vector.tensor_copy(
-            out=w4s[:].rearrange("p a (g t m) -> p (a g) m t", g=N_GROUPS, t=PACK),
-            in_=w4s_raw[:].rearrange("p a (g m t) -> p (a g) m t", g=N_GROUPS, t=PACK),
+            out=w4s_dealt[:].rearrange("p (g t c i) -> p g c t i", g=N_GROUPS, t=PACK, i=16),
+            in_=w4s_raw[:].rearrange("p (g c i t) -> p g c t i", g=N_GROUPS, t=PACK, i=16),
         )
+        for q in range(4):
+            nc.gpsimd.dma_start(
+                out=w4s[32 * q : 32 * q + 4].rearrange("p a n -> p (a n)").bitcast(I32),
+                in_=w4s_dealt[8 * q : 8 * q + 8, :].bitcast(I32),
+            )
 
         h_sb = {}
 
@@ -241,11 +240,14 @@ def tile_list_perimetry_visit_features_kernel(
             follow[b, t] = h2
             cosine[b, t] = cos
 
+        def pick_baseline(b, t, lo, hi, prod):
+            nc.vector.tensor_copy(prod, h_sb[b, t][:].indirect(pos1_sb[:, lo // 16 : hi // 16]))
+
+        def multiply(b, t, lo, hi, prod):
+            nc.vector.tensor_tensor(out=prod, in0=prod, in1=cosine[b, t][:, lo:hi], op=ALU.mult)
+
         def combine(b, t, lo, hi, prod, x32):
             col = b * PACK + t
-            nc.vector.tensor_tensor(
-                prod, h_sb[b, t][:].indirect(pos1_sb[:, lo // 16 : hi // 16]), cosine[b, t][:, lo:hi], ALU.mult
-            )
             nc.vector.scalar_tensor_tensor(
                 out=x32[:, t, :],
                 in0=follow[b, t][:, lo:hi],
@@ -278,22 +280,21 @@ def tile_list_perimetry_visit_features_kernel(
             for g in range(N_GROUPS):
                 y = stage.tile([P, PACK, width], F32, name="stage", align_bytes=64)
                 for t0 in range(0, PACK, 2):
-                    acc = psum.tile([P, 2, width], F32, name="acc2")
-                    for t in range(t0, t0 + 2):
-                        n_cols = slice(g * PASS + t * P, g * PASS + (t + 1) * P)
-                        for b in range(H_PASSES):
-                            codes, scales = operands[b]
+                    acc = psum.tile([P, 2, width], F32, name="acc1" if last else "acc2")
+                    for b in range(H_PASSES):
+                        codes, scales = operands[b]
+                        for t in range(t0, t0 + 2):
+                            n_cols = slice(g * PASS + t * P, g * PASS + (t + 1) * P)
                             nc.tensor.matmul_mx(
                                 out=acc[:, t - t0, :],
                                 lhsT=w4_dealt[:, b, n_cols].bitcast(E2M1X4),
                                 lhsT_scale=w4s[:, b, n_cols],
                                 rhs=codes.bitcast(E4M3X4),
                                 rhs_scale=scales,
-                                start=(b == 0),
-                                stop=(b == H_PASSES - 1),
+                                start=(b == 0 and t == t0),
+                                stop=(b == H_PASSES - 1 and t == t0 + 1),
                             )
-                    evacuate = nc.vector.tensor_copy if last and t0 > 0 else nc.scalar.copy
-                    evacuate(out=y[:, t0 : t0 + 2, :], in_=acc[:])
+                    nc.scalar.copy(out=y[:, t0 : t0 + 2, :], in_=acc[:])
                 nc.sync.dma_start(
                     out=out_0[g * PASS : (g + 1) * PASS, lo:hi].rearrange("(p t) j -> p t j", t=PACK), in_=y[:]
                 )
@@ -321,12 +322,19 @@ def tile_list_perimetry_visit_features_kernel(
             if t + 1 < PACK:
                 pick_follow_up(0, t + 1)
             prod = work.tile([P, PAIRS], F32, name="prod")
-            combine(0, t, 0, PAIRS, prod[:], x32)
+            pick_baseline(0, t, 0, PAIRS, prod[:])
+            multiply(0, t, 0, PAIRS, prod[:])
             if t < K_PASSES:
                 quantise_w1(t, 1)
+            combine(0, t, 0, PAIRS, prod[:], x32)
             if t == K_PASSES - 1:
                 first_stage(1, 0)
                 first_stage(1, 1)
+        w4_dealt = keep.tile([P, H_PASSES, N], U16, name="w4_dealt", align_bytes=64)
+        nc.scalar.copy(
+            out=w4_dealt[:].rearrange("p a (g t c i) -> p (a g) c t i", g=N_GROUPS, t=PACK, i=8),
+            in_=w4_raw[:].bitcast(U16).rearrange("p a (g c i t) -> p (a g) c t i", g=N_GROUPS, t=PACK, i=8),
+        )
         pick_follow_up(1, 0)
         x_codes0, x_scales0 = quantise_x(0, 0, PAIRS, x32)
 
@@ -338,12 +346,20 @@ def tile_list_perimetry_visit_features_kernel(
                 first_stage(1, t + 2)
             if t + 1 < PACK:
                 pick_follow_up(1, t + 1)
-            combine(1, t, lo0, hi0, prods[:, t, :], x32)
+            pick_baseline(1, t, lo0, hi0, prods[:, t, :])
+            if t > 0:
+                combine(1, t - 1, lo0, hi0, prods[:, t - 1, :], x32)
+            multiply(1, t, lo0, hi0, prods[:, t, :])
+        combine(1, PACK - 1, lo0, hi0, prods[:, PACK - 1, :], x32)
         codes, scales = quantise_x(1, lo0, hi0, x32)
         x32 = work.tile([P, PACK, hi1 - lo1], F32, name="x32")
         prods = keep.tile([P, PACK, hi1 - lo1], F32, name="prods")
         for t in range(PACK):
-            combine(1, t, lo1, hi1, prods[:, t, :], x32)
+            pick_baseline(1, t, lo1, hi1, prods[:, t, :])
+            if t > 0:
+                combine(1, t - 1, lo1, hi1, prods[:, t - 1, :], x32)
+            multiply(1, t, lo1, hi1, prods[:, t, :])
+        combine(1, PACK - 1, lo1, hi1, prods[:, PACK - 1, :], x32)
         second_stage(lo0, hi0, ((x_codes0[:, lo0:hi0], x_scales0[:, lo0:hi0]), (codes[:], scales[:])), False)
         codes, scales = quantise_x(1, lo1, hi1, x32)
         second_stage(lo1, hi1, ((x_codes0[:, lo1:hi1], x_scales0[:, lo1:hi1]), (codes[:], scales[:])), True)

import math
from contextlib import ExitStack

import concourse.mybir as mybir

K, H, N, T, S, PAIRS = 1536, 1024, 1024, 2048, 1024, 512
FLOPS = 2 * K * H * S + 2 * H * N * PAIRS

F32 = mybir.dt.float32
BF16 = mybir.dt.bfloat16
I32 = mybir.dt.int32
U32 = mybir.dt.uint32
U16 = mybir.dt.uint16
U8 = mybir.dt.uint8
E4M3X4 = mybir.dt.float8_e4m3fn_x4
E2M1X4 = mybir.dt.float4_e2m1fn_x4
ALU = mybir.AluOpType
ACT = mybir.ActivationFunctionType

P = 128
PACK = 4
PASS = P * PACK
K_PASSES = K // PASS
H_PASSES = H // PASS
N_GROUPS = N // PASS
BANK = 512
SCALE_ROW0 = 10
TINY = 2.0 ** -100
PIECES = ((0, 256), (256, 512))


def tile_list_perimetry_visit_features_kernel(
    tc, tab_words, tab_scales, offs, pos1, pos2, w1, ref, gain, w4_words, w4_scales, out_0, out_1, out_2
):
    nc = tc.nc
    with ExitStack() as ctx:
        keep = ctx.enter_context(tc.tile_pool(name="keep", bufs=1))
        stage = ctx.enter_context(tc.tile_pool(name="stage", bufs=4))
        h_pool = ctx.enter_context(tc.tile_pool(name="h", bufs=8))
        work = ctx.enter_context(tc.tile_pool(name="work", bufs=2))
        picks = ctx.enter_context(tc.tile_pool(name="picks", bufs=4))
        psum = ctx.enter_context(tc.psum_pool(name="psum", bufs=4))

        offs_sb = keep.tile([P, S // 16], U16, name="offs_sb")
        pos1_sb = keep.tile([P, PAIRS // 16], U16, name="pos1_sb")
        pos2_sb = keep.tile([P, PAIRS // 16], U16, name="pos2_sb")
        nc.sync.dma_start(offs_sb[:], offs)
        nc.sync.dma_start(pos2_sb[:], pos2)
        nc.sync.dma_start(pos1_sb[:], pos1)

        ones = stage.tile([P, 1], F32, name="stage", align_bytes=64)
        nc.gpsimd.memset(ones[:], 1.0)
        gain_sb = stage.tile([P, H_PASSES, PACK], F32, name="stage", align_bytes=64)
        nc.sync.dma_start(out=gain_sb[:], in_=gain.rearrange("(b p t) -> p b t", p=P, t=PACK))

        scale_win = keep.tile([P, T], U8, name="scale_win", align_bytes=64)
        scale_got = keep.tile([P, S], U8, name="scale_got", align_bytes=64)
        v_scales = keep.tile([P, K_PASSES, S], U8, name="v_scales", align_bytes=64)
        nc.gpsimd.memset(scale_win[:].bitcast(I32), 0)
        rows = PACK * K_PASSES
        for d in range(4):
            lo = 32 * d + SCALE_ROW0
            nc.sync.dma_start(
                out=scale_win[lo : lo + rows, :].bitcast(I32),
                in_=tab_scales[:, 4 * d : 4 * d + 4, :].rearrange("a r t -> r a t").bitcast(I32),
            )
        nc.vector.memset(v_scales[:].rearrange("p a s -> p (a s)").bitcast(I32), 0)

        nc.vector.tensor_copy(scale_got[:], scale_win[:].indirect(offs_sb[:]))
        for d in range(4):
            lo = 32 * d + SCALE_ROW0
            nc.gpsimd.dma_start(
                out=v_scales[32 * d : 32 * d + 4].rearrange("p a s -> p (a s)").bitcast(I32),
                in_=scale_got[lo : lo + rows, :].bitcast(I32),
            )

        w4s_raw = keep.tile([P, N], U8, name="w4s_raw", align_bytes=64)
        w4s = keep.tile([P, H_PASSES, N], U8, name="w4s", align_bytes=64)
        nc.vector.memset(w4s_raw[:].bitcast(I32), 0)
        nc.gpsimd.dma_start(
            out=w4s_raw[0 : 16 * H_PASSES, :].bitcast(I32), in_=w4_scales.rearrange("a q n -> q a n").bitcast(I32)
        )
        nc.vector.memset(w4s[:].rearrange("p a n -> p (a n)").bitcast(I32), 0)

        w1_codes = {}
        w1_scales = {}
        w1_raw = {}
        w1_grouped = {}

        def load_w1(a, b):
            raw = stage.tile([P, PACK, PASS], F32, name="stage", align_bytes=64)
            nc.sync.dma_start(
                out=raw[:],
                in_=w1[a * PASS : (a + 1) * PASS, b * PASS : (b + 1) * PASS].rearrange("(p j) c -> p j c", j=PACK),
            )
            w1_raw[a, b] = raw

        def round_w1(a, b):
            grouped = picks.tile([P, PACK, P, PACK], BF16, name="w1_grouped", align_bytes=64)
            src = w1_raw[a, b][:].rearrange("p j (m t) -> p m j t", t=PACK)
            dst = grouped[:].rearrange("p t m j -> p m j t")
            nc.scalar.copy(out=dst, in_=src)
            w1_grouped[a, b] = grouped

        def quantise_w1(a, b):
            codes = keep.tile([P, PASS], U32, name="w1_codes_%d_%d" % (a, b), align_bytes=64)
            scales = keep.tile([P, PASS], U8, name="w1_scales_%d_%d" % (a, b), align_bytes=64)
            nc.vector.quantize_mx(
                out=codes[:].bitcast(E4M3X4),
                scales=scales[:],
                in_=w1_grouped[a, b][:].rearrange("p t m j -> p (t m j)"),
            )
            w1_codes[a, b] = codes
            w1_scales[a, b] = scales

        v_words = []
        tabs = []

        def load_table(a):
            tab = stage.tile([P, T], I32, name="stage", align_bytes=64)
            nc.sync.dma_start(out=tab[:], in_=tab_words[a].rearrange("p t i -> p (t i)").bitcast(I32))
            tabs.append(tab)

        load_table(0)
        load_w1(0, 0)
        neg_pi = keep.tile([P, 1], F32, name="neg_pi")
        nc.vector.tensor_scalar(out=neg_pi[:], in0=ones[:], scalar1=-math.pi, scalar2=None, op0=ALU.mult)
        gains = gain_sb[:].rearrange("p b t -> p (b t)")
        cols = H_PASSES * PACK
        sgn = keep.tile([P, cols], F32, name="sgn")
        neg_sgn = keep.tile([P, cols], F32, name="neg_sgn")
        sin_bias = keep.tile([P, cols], F32, name="sin_bias")
        mag = keep.tile([P, cols], F32, name="mag")
        inv_mag = keep.tile([P, cols], F32, name="inv_mag")
        nc.vector.tensor_scalar(out=sgn[:], in0=gains, scalar1=0.0, scalar2=2.0, op0=ALU.is_ge, op1=ALU.mult)
        nc.vector.tensor_scalar(out=neg_sgn[:], in0=sgn[:], scalar1=-1.0, scalar2=1.0, op0=ALU.mult, op1=ALU.add)
        nc.vector.tensor_scalar(out=sgn[:], in0=sgn[:], scalar1=-1.0, scalar2=None, op0=ALU.add)
        nc.vector.tensor_scalar(out=sin_bias[:], in0=neg_sgn[:], scalar1=math.pi / 2, scalar2=None, op0=ALU.mult)
        nc.vector.tensor_tensor(out=mag[:], in0=gains, in1=sgn[:], op=ALU.mult)
        nc.vector.tensor_scalar(out=mag[:], in0=mag[:], scalar1=TINY, scalar2=None, op0=ALU.max)
        nc.vector.reciprocal(out=inv_mag[:], in_=mag[:])

        load_table(1)
        load_w1(1, 0)
        load_table(2)
        load_w1(2, 0)
        for a in range(K_PASSES):
            got = keep.tile([P, S], U32, name="v_words_%d" % a, align_bytes=64)
            nc.vector.tensor_copy(got[:], tabs[a][:].bitcast(U32).indirect(offs_sb[:]))
            v_words.append(got)
            if a < K_PASSES - 1:
                round_w1(a, 0)
                quantise_w1(a, 0)
        last = K_PASSES - 1
        codes = keep.tile([P, PASS], U32, name="w1_codes_last", align_bytes=64)
        scales = keep.tile([P, PASS], U8, name="w1_scales_last", align_bytes=64)
        for half in range(2):
            grouped = keep.tile([P, 2, P, PACK], BF16, name="w1_half_%d" % half, align_bytes=64)
            nc.scalar.copy(
                out=grouped[:].rearrange("p t m j -> p m j t"),
                in_=w1_raw[last, 0][:].rearrange("p j (m t) -> p m j t", t=PACK)[:, :, :, 2 * half : 2 * half + 2],
            )
            half_cols = slice(half * 2 * P, (half + 1) * 2 * P)
            nc.vector.quantize_mx(
                out=codes[:, half_cols].bitcast(E4M3X4),
                scales=scales[:, half_cols],
                in_=grouped[:].rearrange("p t m j -> p (t m j)"),
            )
        w1_codes[last, 0] = codes
        w1_scales[last, 0] = scales

        ref_sb = {}

        def load_ref(b, t0):
            tile = stage.tile([P, 2, S], F32, name="stage", align_bytes=64)
            nc.sync.dma_start(
                out=tile[:],
                in_=ref[b * PASS : (b + 1) * PASS, :].rearrange("(p t) j -> p t j", t=PACK)[:, t0 : t0 + 2, :],
            )
            ref_sb[b, t0] = tile[:, 0, :]
            ref_sb[b, t0 + 1] = tile[:, 1, :]

        load_ref(0, 0)
        load_w1(0, 1)
        load_ref(0, 2)
        load_w1(1, 1)
        load_w1(2, 1)
        load_ref(1, 0)
        w4_raw = stage.tile([P, H_PASSES, N // 2], I32, name="stage", align_bytes=64)
        nc.sync.dma_start(out=w4_raw[:], in_=w4_words.rearrange("a p c -> p a c").bitcast(I32))
        load_ref(1, 2)

        w4s_dealt = keep.tile([P, N], U8, name="w1_half_0", align_bytes=64)
        nc.vector.tensor_copy(
            out=w4s_dealt[:].rearrange("p (g t c i) -> p g c t i", g=N_GROUPS, t=PACK, i=16),
            in_=w4s_raw[:].rearrange("p (g c i t) -> p g c t i", g=N_GROUPS, t=PACK, i=16),
        )
        for q in range(4):
            nc.gpsimd.dma_start(
                out=w4s[32 * q : 32 * q + 4].rearrange("p a n -> p (a n)").bitcast(I32),
                in_=w4s_dealt[8 * q : 8 * q + 8, :].bitcast(I32),
            )

        h_sb = {}

        def first_stage(b, t):
            h = h_pool.tile([P, S], F32, name="h_sb")
            m_cols = slice(t * P, (t + 1) * P)
            for j0 in range(0, S, BANK):
                acc = psum.tile([P, BANK], F32, name="acc1")
                for a in range(K_PASSES):
                    nc.tensor.matmul_mx(
                        out=acc[:],
                        lhsT=w1_codes[a, b][:, m_cols].bitcast(E4M3X4),
                        lhsT_scale=w1_scales[a, b][:, m_cols],
                        rhs=v_words[a][:, j0 : j0 + BANK].bitcast(E4M3X4),
                        rhs_scale=v_scales[:, a, j0 : j0 + BANK],
                        start=(a == 0),
                        stop=(a == K_PASSES - 1),
                    )
                nc.vector.tensor_tensor(
                    out=h[:, j0 : j0 + BANK], in0=acc[:], in1=ref_sb[b, t][:, j0 : j0 + BANK], op=ALU.subtract
                )
            col = b * PACK + t
            nc.scalar.activation(out=h[:], in_=h[:], func=ACT.Abs, scale=mag[:, col : col + 1])
            h_sb[b, t] = h

        follow = {}
        cosine = {}

        def pick_follow_up(b, t):
            col = b * PACK + t
            h2 = picks.tile([P, PAIRS], F32, name="h2")
            nc.vector.tensor_copy(h2[:], h_sb[b, t][:].indirect(pos2_sb[:]))
            cos = picks.tile([P, PAIRS], F32, name="cos")
            nc.scalar.activation(out=cos[:], in_=h2[:], func=ACT.Abs, scale=inv_mag[:, col : col + 1], bias=neg_pi[:])
            nc.scalar.activation(
                out=cos[:], in_=cos[:], func=ACT.Sin, scale=sgn[:, col : col + 1], bias=sin_bias[:, col : col + 1]
            )
            follow[b, t] = h2
            cosine[b, t] = cos

        def pick_baseline(b, t, lo, hi, prod):
            nc.vector.tensor_copy(prod, h_sb[b, t][:].indirect(pos1_sb[:, lo // 16 : hi // 16]))

        def multiply(b, t, lo, hi, prod):
            nc.vector.tensor_tensor(out=prod, in0=prod, in1=cosine[b, t][:, lo:hi], op=ALU.mult)

        def combine(b, t, lo, hi, prod, x32):
            col = b * PACK + t
            nc.vector.scalar_tensor_tensor(
                out=x32[:, t, :],
                in0=follow[b, t][:, lo:hi],
                scalar=neg_sgn[:, col : col + 1],
                in1=prod,
                op0=ALU.mult,
                op1=ALU.add,
            )

        def interleave(engine_copy, dst, src):
            engine_copy(
                out=dst[:].rearrange("p (c i) t -> p c t i", i=PACK),
                in_=src[:].rearrange("p t (c i) -> p c t i", i=PACK),
            )

        def quantise_x(b, lo, hi, x32):
            x16 = work.tile([P, hi - lo, PACK], BF16, name="x16", align_bytes=64)
            interleave(nc.scalar.copy if b == 0 else nc.vector.tensor_copy, x16, x32)
            codes = keep.tile([P, hi - lo], U32, name="x_codes_%d_%d" % (b, lo), align_bytes=64)
            scales = keep.tile([P, hi - lo], U8, name="x_scales_%d_%d" % (b, lo), align_bytes=64)
            nc.vector.quantize_mx(
                out=codes[:].bitcast(E4M3X4), scales=scales[:], in_=x16[:].rearrange("p c t -> p (c t)")
            )
            return codes, scales

        y_scales = keep.tile([P, N_GROUPS, PAIRS], U8, name="y_scales", align_bytes=64)

        def second_stage(lo, hi, operands, last):
            width = hi - lo
            for g in range(N_GROUPS):
                y = stage.tile([P, PACK, width], F32, name="stage", align_bytes=64)
                for t0 in range(0, PACK, 2):
                    acc = psum.tile([P, 2, width], F32, name="acc1" if last else "acc2")
                    for b in range(H_PASSES):
                        codes, scales = operands[b]
                        for t in range(t0, t0 + 2):
                            n_cols = slice(g * PASS + t * P, g * PASS + (t + 1) * P)
                            nc.tensor.matmul_mx(
                                out=acc[:, t - t0, :],
                                lhsT=w4_dealt[:, b, n_cols].bitcast(E2M1X4),
                                lhsT_scale=w4s[:, b, n_cols],
                                rhs=codes.bitcast(E4M3X4),
                                rhs_scale=scales,
                                start=(b == 0 and t == t0),
                                stop=(b == H_PASSES - 1 and t == t0 + 1),
                            )
                    nc.scalar.copy(out=y[:, t0 : t0 + 2, :], in_=acc[:])
                nc.sync.dma_start(
                    out=out_0[g * PASS : (g + 1) * PASS, lo:hi].rearrange("(p t) j -> p t j", t=PACK), in_=y[:]
                )
                y16 = work.tile([P, width, PACK], BF16, name="y16", align_bytes=64)
                interleave(nc.vector.tensor_copy if last else nc.scalar.copy, y16, y)
                y_codes = work.tile([P, width], U32, name="y_codes", align_bytes=64)
                nc.vector.quantize_mx(
                    out=y_codes[:].bitcast(E4M3X4),
                    scales=y_scales[:, g, lo:hi],
                    in_=y16[:].rearrange("p c t -> p (c t)"),
                )
                nc.sync.dma_start(
                    out=out_1[g].rearrange("p m t -> p (m t)").bitcast(I32)[:, lo:hi], in_=y_codes[:].bitcast(I32)
                )

        x32 = work.tile([P, PACK, PAIRS], F32, name="x32")
        first_stage(0, 0)
        first_stage(0, 1)
        pick_follow_up(0, 0)
        for t in range(PACK):
            if t < K_PASSES:
                round_w1(t, 1)
            if t + 2 < PACK:
                first_stage(0, t + 2)
            if t + 1 < PACK:
                pick_follow_up(0, t + 1)
            prod = work.tile([P, PAIRS], F32, name="prod")
            pick_baseline(0, t, 0, PAIRS, prod[:])
            multiply(0, t, 0, PAIRS, prod[:])
            if t < K_PASSES:
                quantise_w1(t, 1)
            combine(0, t, 0, PAIRS, prod[:], x32)
            if t == K_PASSES - 1:
                first_stage(1, 0)
                first_stage(1, 1)
        w4_dealt = keep.tile([P, H_PASSES, N], U16, name="w4_dealt", align_bytes=64)
        nc.scalar.copy(
            out=w4_dealt[:].rearrange("p a (g t c i) -> p (a g) c t i", g=N_GROUPS, t=PACK, i=8),
            in_=w4_raw[:].bitcast(U16).rearrange("p a (g c i t) -> p (a g) c t i", g=N_GROUPS, t=PACK, i=8),
        )
        pick_follow_up(1, 0)
        x_codes0, x_scales0 = quantise_x(0, 0, PAIRS, x32)

        (lo0, hi0), (lo1, hi1) = PIECES
        x32 = work.tile([P, PACK, hi0 - lo0], F32, name="x32")
        prods = keep.tile([P, PACK, hi0 - lo0], F32, name="prods")
        for t in range(PACK):
            if t + 2 < PACK:
                first_stage(1, t + 2)
            if t + 1 < PACK:
                pick_follow_up(1, t + 1)
            pick_baseline(1, t, lo0, hi0, prods[:, t, :])
            if t > 0:
                combine(1, t - 1, lo0, hi0, prods[:, t - 1, :], x32)
            multiply(1, t, lo0, hi0, prods[:, t, :])
        combine(1, PACK - 1, lo0, hi0, prods[:, PACK - 1, :], x32)
        codes, scales = quantise_x(1, lo0, hi0, x32)
        x32 = work.tile([P, PACK, hi1 - lo1], F32, name="x32")
        prods = keep.tile([P, PACK, hi1 - lo1], F32, name="prods")
        for t in range(PACK):
            pick_baseline(1, t, lo1, hi1, prods[:, t, :])
            if t > 0:
                combine(1, t - 1, lo1, hi1, prods[:, t - 1, :], x32)
            multiply(1, t, lo1, hi1, prods[:, t, :])
        combine(1, PACK - 1, lo1, hi1, prods[:, PACK - 1, :], x32)
        second_stage(lo0, hi0, ((x_codes0[:, lo0:hi0], x_scales0[:, lo0:hi0]), (codes[:], scales[:])), False)
        codes, scales = quantise_x(1, lo1, hi1, x32)
        second_stage(lo1, hi1, ((x_codes0[:, lo1:hi1], x_scales0[:, lo1:hi1]), (codes[:], scales[:])), True)

        for q in range(4):
            queue = nc.sync if q % 2 == 0 else nc.scalar
            queue.dma_start(
                out=out_2[:, 4 * q : 4 * q + 4, :].rearrange("g r m -> r g m").bitcast(I32),
                in_=y_scales[32 * q : 32 * q + 4].rearrange("p g m -> p (g m)").bitcast(I32),
            )
